import numpy as np
import ml_dtypes


def mxq(x, axis, fmt="e4m3"):
    dtype, down = {"e4m3": (ml_dtypes.float8_e4m3fn, 7), "e5m2": (ml_dtypes.float8_e5m2, 14)}[fmt]
    v = np.moveaxis(np.asarray(x, np.float32).astype(ml_dtypes.bfloat16).astype(np.float64), axis, -1)
    blocks = v.reshape(v.shape[:-1] + (-1, 32))
    amax = np.abs(blocks).max(-1, keepdims=True)
    byte = np.maximum(np.where(amax > 0, np.frexp(amax)[1] - 1 + 127, 0) - down, 1)
    scale = np.exp2(byte - 127.0)
    codes = (blocks / scale).astype(np.float32).astype(dtype).astype(np.float64)
    return np.moveaxis((codes * scale).reshape(v.shape), -1, axis)


WIDE = False


def mx_kscale(k):
    if not WIDE:
        return np.ones(k)
    levels = np.array([10, -10, 5, -5, 0])
    if k % 512:
        return np.exp2(np.random.permutation(np.resize(levels, k // 32))).repeat(32)
    a = np.empty((k // 512, 16))
    for p in range(k // 512):
        a[p, :8] = np.random.permutation(np.resize(levels, 8))
        for g in range(8):
            far = levels[np.abs(levels - a[p, g]) >= 10]
            a[p, g + 8] = far[np.random.randint(len(far))]
    return np.exp2(a.ravel()).repeat(32)


def f64(x):
    return np.asarray(x).astype(np.float64)


def striped(idx):
    return np.tile(idx.reshape(-1, 16).T, (8, 1)).astype(np.uint16)


def unstriped(offs):
    return offs[:16].T.reshape(-1).astype(np.int64)


E2M1 = np.array([0.0, 0.5, 1.0, 1.5, 2.0, 3.0, 4.0, 6.0, -0.0, -0.5, -1.0, -1.5, -2.0, -3.0, -4.0, -6.0])


def pack_weight(w, fmt):
    k, n = w.shape
    w = f64(np.asarray(w, np.float32).astype(ml_dtypes.bfloat16)).reshape(k // 32, 32, n)
    amax = np.abs(w).max(1)
    if fmt == "e4m3":
        byte = np.frexp(amax)[1] - 1 + 127 - 7
    else:
        mant, ex = np.frexp(amax / 6.0)
        byte = np.where(mant > 0.5, ex, ex - 1) + 127
    byte = np.clip(np.where(amax > 0, byte, 1), 1, 254)
    scaled = (w * np.exp2(127.0 - byte)[:, None, :]).reshape(k, n).astype(np.float32)
    by_word = np.ascontiguousarray(scaled.reshape(k // 512, 128, 4, n).transpose(0, 1, 3, 2))
    if fmt == "e4m3":
        words = by_word.astype(ml_dtypes.float8_e4m3fn).view(np.uint8)
    else:
        c = by_word.astype(ml_dtypes.float4_e2m1fn).view(np.uint8) & 0xF
        words = (c[..., 0::2] | (c[..., 1::2] << 4)).reshape(k // 512, 128, 2 * n)
    return np.ascontiguousarray(words), np.ascontiguousarray(byte.astype(np.uint8).reshape(k // 512, 16, n))


def unpack_weight(words, scales, fmt):
    g, _, n = scales.shape
    words = np.ascontiguousarray(words).reshape(g, 128, n, -1)
    if fmt == "e4m3":
        vals = words.view(ml_dtypes.float8_e4m3fn).astype(np.float64)
    else:
        nib = np.empty((g, 128, n, 4), np.uint8)
        nib[..., 0::2] = words & 0xF
        nib[..., 1::2] = words >> 4
        vals = E2M1[nib]
    vals = vals * np.repeat(np.exp2(scales.astype(np.float64) - 127.0), 8, axis=1)[..., None]
    return vals.transpose(0, 1, 3, 2).reshape(g * 512, n)


def gelu(v):
    return 0.5 * v * (1.0 + np.tanh(np.sqrt(2.0 / np.pi) * (v + 0.044715 * v**3)))


K, L, H, T, T3, S, T2, P = 1024, 512, 512, 2048, 1024, 512, 2048, 1024

def setup_inputs():
    n = np.random.standard_normal
    s, s2, u = mx_kscale(K)[:, None], mx_kscale(L)[:, None], mx_kscale(H)[:, None]
    perm = np.random.permutation(T2)
    d = {}
    d["tab_words"], d["tab_scales"] = pack_weight(n((K, T)) * s, "e4m3")
    d["tab2_words"], d["tab2_scales"] = pack_weight(n((L, T3)) * s2, "e4m3")
    d["offs"] = striped(np.random.permutation(T)[:S])
    d["offs2"] = striped(np.random.permutation(T3)[:S])
    d["offs3"] = striped(perm[:S])
    d["offs4"] = striped(perm[S:2 * S])
    d["offs5"] = striped(np.random.permutation(T2)[:P])
    d["w1"] = (0.55 * n((K, H)) / K**0.5 / s).astype(np.float32)
    d["w2_words"], d["w2_scales"] = pack_weight(0.3 * n((K, H)) / K**0.5 / s, "e2m1")
    d["w3"] = (n((L, H)) / L**0.5 / s2).astype(np.float32)
    d["w4_words"], d["w4_scales"] = pack_weight(n((L, H)) / L**0.5 / s2, "e4m3")
    d["w5"] = (0.6 * n((L, H)) / L**0.5 / s2).astype(np.float32)
    d["w6_words"], d["w6_scales"] = pack_weight(2.3 * n((H, H)) / H**0.5 / u, "e2m1")
    d["wg1"] = np.exp(0.3 * n((128, S))).astype(np.float32)
    d["wg2"] = np.exp(0.3 * n((128, S))).astype(np.float32)
    d["page0"] = (0.5 * n((H, T2))).astype(np.float32)
    d["gr"] = (np.exp(0.3 * n(H)) * u[:, 0]).astype(np.float32)
    return d

def reference(tab_words, tab_scales, tab2_words, tab2_scales, offs, offs2, offs3, offs4, offs5, w1, w2_words, w2_scales, w3, w4_words, w4_scales, w5, w6_words, w6_scales, wg1, wg2, page0, gr):
    v = unpack_weight(tab_words, tab_scales, "e4m3")[:, unstriped(offs)]
    v2 = unpack_weight(tab2_words, tab2_scales, "e4m3")[:, unstriped(offs2)]
    a = mxq(f64(w1), 0, "e4m3").T @ v
    b = unpack_weight(w2_words, w2_scales, "e2m1").T @ v
    h1 = np.sin(a) - b
    c = mxq(f64(w3), 0, "e4m3").T @ v2
    d = unpack_weight(w4_words, w4_scales, "e4m3").T @ v2
    e = mxq(f64(w5), 0, "e4m3").T @ v2
    h2 = np.maximum(c, d) * e
    page = f64(page0).copy()
    page[:, unstriped(offs3)] = np.tile(f64(wg1), (H // 128, 1)) * h1
    page[:, unstriped(offs4)] = np.tile(f64(wg2), (H // 128, 1)) * h2
    x = page[:, unstriped(offs5)]
    z = x * f64(gr)[:, None]
    y = unpack_weight(w6_words, w6_scales, "e2m1").T @ mxq(z, 0, "e4m3")
    return np.tanh(y) * x

@@ -1,0 +1,293 @@
+import math
+from contextlib import ExitStack
+
+import concourse.mybir as mybir
+from concourse.masks import make_identity
+
+K, L, H, T, T3, S, T2, NREAD = 1024, 512, 512, 2048, 1024, 512, 2048, 1024
+FLOPS = 2 * (2 * K * H * S + 3 * L * H * S + H * H * NREAD)
+
+F32 = mybir.dt.float32
+BF16 = mybir.dt.bfloat16
+I32 = mybir.dt.int32
+U32 = mybir.dt.uint32
+U16 = mybir.dt.uint16
+U8 = mybir.dt.uint8
+FP8X4 = mybir.dt.float8_e4m3fn_x4
+FP4X4 = mybir.dt.float4_e2m1fn_x4
+ALU = mybir.AluOpType
+ACT = mybir.ActivationFunctionType
+
+P = 128
+PACK = 4
+QUAD = 32
+CHUNK = 256
+ROUNDER = 1.5 * 2.0**23
+
+
+def tile_list_hub_wear_board_kernel(
+    tc, tab_words, tab_scales, tab2_words, tab2_scales, offs, offs2, offs3, offs4, offs5,
+    w1, w2_words, w2_scales, w3, w4_words, w4_scales, w5, w6_words, w6_scales, wg1, wg2, page0, gr, out,
+):
+    nc = tc.nc
+    with ExitStack() as ctx:
+        keep = ctx.enter_context(tc.tile_pool(name="keep", bufs=1))
+        work = ctx.enter_context(tc.tile_pool(name="work", bufs=4))
+        psum = ctx.enter_context(tc.psum_pool(name="psum", bufs=7))
+
+        def bank(name):
+            return psum.tile([P, 512], F32, name=name, tag="bank")
+
+        def load_list(src, name):
+            tile = keep.tile(list(src.shape), U16, name=name)
+            nc.sync.dma_start(tile[:], src)
+            return tile
+
+        def load_words(src, name, queue):
+            tile = keep.tile([P, src.shape[1] // 4], I32, name=name, align_bytes=64)
+            queue.dma_start(tile[:], src.bitcast(I32))
+            return tile
+
+        def scale_tile(src, name):
+            tile = keep.tile([P, src.shape[0], src.shape[2]], U8, name=name, align_bytes=64)
+            nc.vector.memset(tile[:].bitcast(I32), 0)
+            return tile
+
+        def load_scales(tile, src, queue):
+            for quad in range(4):
+                queue.dma_start(
+                    tile[QUAD * quad : QUAD * quad + 4].bitcast(I32),
+                    src[:, 4 * quad : 4 * quad + 4, :].rearrange("a q c -> q a c").bitcast(I32),
+                )
+
+        def load_weight(rows, name):
+            tile = keep.tile([P, PACK, H], F32, name=name)
+            nc.sync.dma_start(tile[:], rows.rearrange("(p i) c -> p i c", i=PACK))
+            return tile
+
+        def load_gain(src, t, name):
+            tile = keep.tile([P, S], F32, name="%s_%d" % (name, t))
+            rows = src.rearrange("(q t) j -> t q j", t=PACK)[t]
+            for quad in range(4):
+                nc.sync.dma_start(tile[QUAD * quad : QUAD * (quad + 1)], rows)
+            return tile
+
+        def load_page(t):
+            tile = keep.tile([P, T2], F32, name="page%d" % t)
+            nc.sync.dma_start(tile[:], page0.rearrange("(p t) c -> t p c", t=PACK)[t])
+            return tile
+
+        warm = keep.tile([P, 2], F32, name="warm")
+        nc.vector.memset(warm[:, 0:1], 0.0)
+        nc.scalar.activation(warm[:, 1:2], warm[:, 0:1], ACT.Silu)
+
+        v2_scale_tab = scale_tile(tab2_scales, "v2_scale_tab")
+        w4_scale_raw = scale_tile(w4_scales, "w4_scale_raw")
+        v_scale_tab = scale_tile(tab_scales, "v_scale_tab")
+        w6_scale_raw = scale_tile(w6_scales, "w6_scale_raw")
+        w2_scale = scale_tile(w2_scales, "w2_scale")
+
+        load_scales(v_scale_tab, tab_scales, nc.gpsimd)
+
+        idx2 = load_list(offs2, "idx2")
+        idx = load_list(offs, "idx")
+        v2_word_tab = load_words(tab2_words[0].rearrange("p c i -> p (c i)"), "v2_word_tab", nc.sync)
+        w4_word_raw = load_words(w4_words[0].rearrange("p c i -> p (c i)"), "w4_word_raw", nc.sync)
+        load_scales(v2_scale_tab, tab2_scales, nc.sync)
+        w3_raw = load_weight(w3, "w3_raw")
+        load_scales(w4_scale_raw, w4_scales, nc.sync)
+        w5_raw = load_weight(w5, "w5_raw")
+        page = [load_page(0)]
+        gain2 = [load_gain(wg2, 0, "gain2")]
+        idx4 = load_list(offs4, "idx4")
+        v_word_tab = [
+            load_words(tab_words[a].rearrange("p c i -> p (c i)"), "v_word_tab%d" % a, nc.sync) for a in range(2)
+        ]
+        w1_raw = [load_weight(w1[512 * a : 512 * (a + 1), :], "w1_raw%d" % a) for a in range(2)]
+        w2_word = [load_words(w2_words[a], "w2_word%d" % a, nc.sync) for a in range(2)]
+        load_scales(w2_scale, w2_scales, nc.sync)
+        for t in range(1, PACK):
+            gain2.append(load_gain(wg2, t, "gain2"))
+            page.append(load_page(t))
+        w6_word_raw = load_words(w6_words[0], "w6_word_raw", nc.sync)
+        load_scales(w6_scale_raw, w6_scales, nc.sync)
+        idx3 = load_list(offs3, "idx3")
+        idx5 = load_list(offs5, "idx5")
+        gr_col = keep.tile([P, PACK], F32, name="gr_col")
+        nc.sync.dma_start(gr_col[:], gr.rearrange("(p t) -> p t", t=PACK))
+        gain1 = [load_gain(wg1, t, "gain1") for t in range(PACK)]
+
+        ident = keep.tile([P, P], F32, name="ident")
+        make_identity(nc, ident[:])
+
+        def gather_words(table, lst, name):
+            tile = keep.tile([P, S], U32, name=name, align_bytes=64)
+            nc.vector.tensor_copy(tile[:], table[:].bitcast(U32).indirect(lst[:]))
+            return tile
+
+        def gather_scales(table, a, lst, name):
+            tile = keep.tile([P, S], U8, name=name, align_bytes=64)
+            nc.vector.tensor_copy(tile[:], table[:, a, :].indirect(lst[:]))
+            return tile
+
+        def deal_scales(engine, raw, name):
+            tile = keep.tile([P, H], U8, name=name, align_bytes=64)
+            engine.tensor_copy(
+                tile[:].rearrange("p (t m) -> p t m", t=PACK),
+                raw[:, 0, :].rearrange("p (m t) -> p t m", t=PACK),
+            )
+            return tile
+
+        def round_weight(raw, tag):
+            tile = keep.tile([P, PACK * H], BF16, name="rounded", tag=tag, align_bytes=64)
+            dst = tile[:].rearrange("p (t m i) -> p m i t", t=PACK, i=PACK)
+            src = raw[:].rearrange("p i (m t) -> p m i t", t=PACK)
+            nc.scalar.copy(dst, src)
+            return tile
+
+        def quantize(rounded, width, name):
+            codes = keep.tile([P, width], U32, name=name + "_codes", align_bytes=64)
+            scales = keep.tile([P, width], U8, name=name + "_scales", align_bytes=64)
+            nc.vector.quantize_mx(out=codes[:].bitcast(FP8X4), scales=scales[:], in_=rounded)
+            return codes, scales
+
+        v2_scale = gather_scales(v2_scale_tab, 0, idx2, "v2_scale")
+        v2_word = gather_words(v2_word_tab, idx2, "v2_word")
+        w4_word = keep.tile([P, H], I32, name="w4_word", align_bytes=64)
+        nc.vector.tensor_copy(
+            w4_word[:].rearrange("p (t m) -> p m t", t=PACK),
+            w4_word_raw[:].rearrange("p (m t) -> p m t", t=PACK),
+        )
+        w4_scale = deal_scales(nc.vector, w4_scale_raw, "w4_scale")
+        w3_q = quantize(round_weight(w3_raw, "rounded0")[:], H, "w3")
+        w5_q = quantize(round_weight(w5_raw, "rounded1")[:], H, "w5")
+
+        def product_v2(weight, t, name):
+            acc = bank(name)
+            cols = slice(P * t, P * (t + 1))
+            nc.tensor.matmul_mx(
+                out=acc[:], lhsT=weight[0][:, cols].bitcast(FP8X4), lhsT_scale=weight[1][:, cols],
+                rhs=v2_word[:].bitcast(FP8X4), rhs_scale=v2_scale[:], start=True, stop=True,
+            )
+            return acc
+
+        def place_h2(t, h2):
+            nc.vector.tensor_tensor(h2, e_acc[t][:], larger[t][:], ALU.mult)
+            nc.vector.tensor_tensor(page[t][:].indirect(idx4[:]), h2, gain2[t][:], ALU.mult)
+
+        e_acc, larger = [], []
+        for t in range(PACK):
+            c_acc = product_v2(w3_q, t, "c_acc")
+            d_acc = product_v2((w4_word, w4_scale), t, "d_acc")
+            e_acc.append(product_v2(w5_q, t, "e_acc"))
+            c_sb = work.tile([P, S], F32, name="c_sb", bufs=2)
+            nc.scalar.copy(c_sb[:], c_acc[:])
+            larger.append(work.tile([P, S], F32, name="larger"))
+            nc.vector.tensor_tensor(larger[t][:], d_acc[:], c_sb[:], ALU.max)
+            if t == 0:
+                h2_first = keep.tile([P, S], F32, name="h2_first")
+                place_h2(0, h2_first[:])
+
+        v_scale = [gather_scales(v_scale_tab, a, idx, "v_scale%d" % a) for a in range(2)]
+        w6_scale = deal_scales(nc.gpsimd, w6_scale_raw, "w6_scale")
+        w6_word = keep.tile([P, 2 * H], U8, name="w6_word", align_bytes=64)
+        nc.gpsimd.tensor_copy(
+            w6_word[:].rearrange("p (t m b) -> p t m b", t=PACK, b=2),
+            w6_word_raw[:].bitcast(U8).rearrange("p (m t b) -> p t m b", t=PACK, b=2),
+        )
+        v_word = [gather_words(v_word_tab[a], idx, "v_word%d" % a) for a in range(2)]
+        w1_q = [quantize(round_weight(w1_raw[a], "rounded%d" % a)[:], H, "w1_%d" % a) for a in range(2)]
+
+        neg_b = []
+        for jc in range(S // P):
+            b_acc = bank("b_acc")
+            cols = slice(P * jc, P * (jc + 1))
+            for a in range(2):
+                nc.tensor.matmul_mx(
+                    out=b_acc[:], lhsT=v_word[a][:, cols].bitcast(FP8X4), lhsT_scale=v_scale[a][:, cols],
+                    rhs=w2_word[a][:].bitcast(U8).bitcast(FP4X4), rhs_scale=w2_scale[:, a, :],
+                    start=(a == 0), stop=(a == 1),
+                )
+            tile = work.tile([P, H], F32, name="neg_b", tag="neg_b_then_z", align_bytes=64)
+            nc.scalar.activation(
+                tile[:].rearrange("j (t m) -> j t m", t=PACK),
+                b_acc[:].rearrange("j (m t) -> j t m", t=PACK), ACT.Copy, scale=-1.0,
+            )
+            neg_b.append(tile)
+
+        h2_rest = keep.tile([P, PACK - 1, S], F32, name="h2_rest", tag="rounded1", align_bytes=64)
+        for t in range(1, PACK):
+            place_h2(t, h2_rest[:, t - 1, :])
+
+        def add_transposed(dst, first, second):
+            nc.tensor.matmul(dst, first, ident[:], is_transpose=True, start=True, stop=False)
+            nc.tensor.matmul(dst, second, ident[:], is_transpose=True, start=False, stop=True)
+
+        h1 = []
+        for t in range(PACK):
+            a_acc = psum.tile([P, S], F32, name="a_acc", bufs=1)
+            cols = slice(P * t, P * (t + 1))
+            for a in range(2):
+                nc.tensor.matmul_mx(
+                    out=a_acc[:], lhsT=w1_q[a][0][:, cols].bitcast(FP8X4), lhsT_scale=w1_q[a][1][:, cols],
+                    rhs=v_word[a][:].bitcast(FP8X4), rhs_scale=v_scale[a][:], start=(a == 0), stop=(a == 1),
+                )
+            turns = work.tile([P, S], F32, name="turns", bufs=2)
+            nc.scalar.activation(turns[:], a_acc[:], ACT.Copy, scale=1.0 / (2.0 * math.pi))
+            whole = work.tile([P, S], U32, name="whole", bufs=2)
+            nc.scalar.activation(whole[:], turns[:], ACT.Copy, bias=ROUNDER)
+            neg_whole = work.tile([P, S], F32, name="neg_whole", bufs=1)
+            nc.scalar.activation(neg_whole[:], whole[:], ACT.Copy, scale=-1.0, bias=ROUNDER)
+            frac_acc = bank("frac_acc")
+            for jc in range(S // P):
+                blk = slice(P * jc, P * (jc + 1))
+                add_transposed(frac_acc[:, blk], turns[:, blk], neg_whole[:, blk])
+            sine = work.tile([P, S], F32, name="sine", bufs=2)
+            nc.scalar.activation(sine[:], frac_acc[:], ACT.Sin, scale=2.0 * math.pi)
+            h1_acc = bank("h1_acc")
+            for jc in range(S // P):
+                blk = slice(P * jc, P * (jc + 1))
+                add_transposed(h1_acc[:, blk], sine[:, blk], neg_b[jc][:, cols])
+            h1_t = work.tile([P, S], F32, name="h1")
+            nc.scalar.copy(h1_t[:], h1_acc[:])
+            h1.append(h1_t)
+
+        chunks = NREAD // CHUNK
+        x = [keep.tile([P, NREAD], F32, name="x%d" % t) for t in range(PACK)]
+        z = [work.tile([P, CHUNK, PACK], BF16, name="z", tag="neg_b_then_z", align_bytes=64) for c in range(chunks)]
+        for t in range(PACK):
+            nc.vector.tensor_tensor(page[t][:].indirect(idx3[:]), h1[t][:], gain1[t][:], ALU.mult)
+            piece = CHUNK if t == PACK - 1 else NREAD
+            for j0 in range(0, NREAD, piece):
+                nc.vector.tensor_copy(
+                    x[t][:, j0 : j0 + piece], page[t][:].indirect(idx5[:, j0 // 16 : (j0 + piece) // 16])
+                )
+            for c in range(chunks):
+                nc.scalar.activation(
+                    z[c][:, :, t], x[t][:, CHUNK * c : CHUNK * (c + 1)], ACT.Copy, scale=gr_col[:, t : t + 1]
+                )
+
+        z_codes = [keep.tile([P, 512], U32, name="z_codes%d" % h, align_bytes=64) for h in range(2)]
+        z_scales = [keep.tile([P, 512], U8, name="z_scales%d" % h, align_bytes=64) for h in range(2)]
+        for c in range(chunks):
+            cols = slice(CHUNK * (c % 2), CHUNK * (c % 2 + 1))
+            nc.vector.quantize_mx(
+                out=z_codes[c // 2][:, cols].bitcast(FP8X4), scales=z_scales[c // 2][:, cols],
+                in_=z[c][:].rearrange("p j t -> p (j t)"),
+            )
+
+        out_rows = out.rearrange("(p t) j -> t p j", t=PACK)
+        for h in range(2):
+            cols = slice(512 * h, 512 * (h + 1))
+            for t in range(PACK):
+                y_acc = bank("y_acc")
+                nc.tensor.matmul_mx(
+                    out=y_acc[:],
+                    lhsT=w6_word[:, 2 * P * t : 2 * P * (t + 1)].bitcast(FP4X4),
+                    lhsT_scale=w6_scale[:, P * t : P * (t + 1)],
+                    rhs=z_codes[h][:].bitcast(FP8X4), rhs_scale=z_scales[h][:], start=True, stop=True,
+                )
+                result = keep.tile([P, 512], F32, name="result%d_%d" % (h, t))
+                nc.scalar.activation(result[:], y_acc[:], ACT.Tanh)
+                nc.vector.tensor_tensor(result[:], result[:], x[t][:, cols], ALU.mult)
+                nc.sync.dma_start(out_rows[t][:, cols], result[:])

@@ -33,7 +33,7 @@ def tile_list_hub_wear_board_kernel(
     with ExitStack() as ctx:
         keep = ctx.enter_context(tc.tile_pool(name="keep", bufs=1))
         work = ctx.enter_context(tc.tile_pool(name="work", bufs=4))
-        psum = ctx.enter_context(tc.psum_pool(name="psum", bufs=7))
+        psum = ctx.enter_context(tc.psum_pool(name="psum", bufs=5))
 
         def bank(name):
             return psum.tile([P, 512], F32, name=name, tag="bank")
@@ -60,17 +60,17 @@ def tile_list_hub_wear_board_kernel(
                     src[:, 4 * quad : 4 * quad + 4, :].rearrange("a q c -> q a c").bitcast(I32),
                 )
 
-        def load_weight(rows, name):
-            tile = keep.tile([P, PACK, H], F32, name=name)
-            nc.sync.dma_start(tile[:], rows.rearrange("(p i) c -> p i c", i=PACK))
+        def load_weight(rows, c0, c1, name):
+            tile = keep.tile([P, PACK, c1 - c0], F32, name=name, align_bytes=64)
+            nc.sync.dma_start(tile[:], rows.rearrange("(p i) c -> p i c", i=PACK)[:, :, c0:c1])
             return tile
 
-        def load_gain(src, t, name):
-            tile = keep.tile([P, S], F32, name="%s_%d" % (name, t))
-            rows = src.rearrange("(q t) j -> t q j", t=PACK)[t]
+        def load_gain(src, t0, t1, name):
+            tile = keep.tile([P, t1 - t0, S], F32, name="%s_%d" % (name, t0))
+            rows = src.rearrange("(q t) j -> q t j", t=PACK)[:, t0:t1, :]
             for quad in range(4):
                 nc.sync.dma_start(tile[QUAD * quad : QUAD * (quad + 1)], rows)
-            return tile
+            return [tile[:, n, :] for n in range(t1 - t0)]
 
         def load_page(t):
             tile = keep.tile([P, T2], F32, name="page%d" % t)
@@ -81,41 +81,54 @@ def tile_list_hub_wear_board_kernel(
         nc.vector.memset(warm[:, 0:1], 0.0)
         nc.scalar.activation(warm[:, 1:2], warm[:, 0:1], ACT.Silu)
 
+        v_scale_tab = keep.tile([P, 1, T], U8, name="v_scale_tab", align_bytes=64)
+        nc.vector.memset(v_scale_tab[:].bitcast(I32), 0)
         v2_scale_tab = scale_tile(tab2_scales, "v2_scale_tab")
         w4_scale_raw = scale_tile(w4_scales, "w4_scale_raw")
-        v_scale_tab = scale_tile(tab_scales, "v_scale_tab")
         w6_scale_raw = scale_tile(w6_scales, "w6_scale_raw")
         w2_scale = scale_tile(w2_scales, "w2_scale")
+        v_scale_second = keep.tile([P, S], U8, name="v_scale_second", align_bytes=64)
+        nc.vector.memset(v_scale_second[:].bitcast(I32), 0)
 
-        load_scales(v_scale_tab, tab_scales, nc.gpsimd)
+        for quad in range(4):
+            nc.gpsimd.dma_start(
+                v_scale_tab[QUAD * quad : QUAD * quad + 8, 0, :].bitcast(I32),
+                tab_scales[:, 4 * quad : 4 * quad + 4, :].bitcast(I32),
+            )
 
         idx2 = load_list(offs2, "idx2")
         idx = load_list(offs, "idx")
+        w3_raw = [load_weight(w3, 0, H, "w3_raw")]
+        load_scales(v2_scale_tab, tab2_scales, nc.sync)
         v2_word_tab = load_words(tab2_words[0].rearrange("p c i -> p (c i)"), "v2_word_tab", nc.sync)
         w4_word_raw = load_words(w4_words[0].rearrange("p c i -> p (c i)"), "w4_word_raw", nc.sync)
-        load_scales(v2_scale_tab, tab2_scales, nc.sync)
-        w3_raw = load_weight(w3, "w3_raw")
+        w5_raw = [load_weight(w5, 0, H // 2, "w5_raw_left")]
         load_scales(w4_scale_raw, w4_scales, nc.sync)
-        w5_raw = load_weight(w5, "w5_raw")
+        w5_raw.append(load_weight(w5, H // 2, H, "w5_raw_right"))
         page = [load_page(0)]
-        gain2 = [load_gain(wg2, 0, "gain2")]
+        gain2 = load_gain(wg2, 0, 1, "gain2")
         idx4 = load_list(offs4, "idx4")
         v_word_tab = [
             load_words(tab_words[a].rearrange("p c i -> p (c i)"), "v_word_tab%d" % a, nc.sync) for a in range(2)
         ]
-        w1_raw = [load_weight(w1[512 * a : 512 * (a + 1), :], "w1_raw%d" % a) for a in range(2)]
-        w2_word = [load_words(w2_words[a], "w2_word%d" % a, nc.sync) for a in range(2)]
+        w1_raw = [[load_weight(w1[0:512, :], 0, H, "w1_raw0")]]
+        w2_word = keep.tile([P, 2, 2 * H], U8, name="w2_word", align_bytes=64)
+        nc.sync.dma_start(w2_word[:].bitcast(I32), w2_words.rearrange("a p c -> p a c").bitcast(I32))
         load_scales(w2_scale, w2_scales, nc.sync)
+        w1_raw.append([
+            load_weight(w1[512:1024, :], 0, H // 2, "w1_raw1_left"),
+            load_weight(w1[512:1024, :], H // 2, H, "w1_raw1_right"),
+        ])
         for t in range(1, PACK):
-            gain2.append(load_gain(wg2, t, "gain2"))
             page.append(load_page(t))
-        w6_word_raw = load_words(w6_words[0], "w6_word_raw", nc.sync)
-        load_scales(w6_scale_raw, w6_scales, nc.sync)
+            gain2 = gain2 + load_gain(wg2, t, t + 1, "gain2")
         idx3 = load_list(offs3, "idx3")
         idx5 = load_list(offs5, "idx5")
         gr_col = keep.tile([P, PACK], F32, name="gr_col")
         nc.sync.dma_start(gr_col[:], gr.rearrange("(p t) -> p t", t=PACK))
-        gain1 = [load_gain(wg1, t, "gain1") for t in range(PACK)]
+        gain1 = load_gain(wg1, 0, 2, "gain1") + load_gain(wg1, 2, 3, "gain1") + load_gain(wg1, 3, 4, "gain1")
+        w6_word_raw = load_words(w6_words[0], "w6_word_raw", nc.sync)
+        load_scales(w6_scale_raw, w6_scales, nc.sync)
 
         ident = keep.tile([P, P], F32, name="ident")
         make_identity(nc, ident[:])
@@ -125,14 +138,14 @@ def tile_list_hub_wear_board_kernel(
             nc.vector.tensor_copy(tile[:], table[:].bitcast(U32).indirect(lst[:]))
             return tile
 
-        def gather_scales(table, a, lst, name):
-            tile = keep.tile([P, S], U8, name=name, align_bytes=64)
+        def gather_scales(table, a, lst, tag):
+            tile = keep.tile([P, S], U8, name="picked_scales", tag=tag, align_bytes=64)
             nc.vector.tensor_copy(tile[:], table[:, a, :].indirect(lst[:]))
             return tile
 
-        def deal_scales(engine, raw, name):
+        def deal_scales(raw, name):
             tile = keep.tile([P, H], U8, name=name, align_bytes=64)
-            engine.tensor_copy(
+            nc.vector.tensor_copy(
                 tile[:].rearrange("p (t m) -> p t m", t=PACK),
                 raw[:, 0, :].rearrange("p (m t) -> p t m", t=PACK),
             )
@@ -141,12 +154,13 @@ def tile_list_hub_wear_board_kernel(
         def round_weight(raw, tag):
             tile = keep.tile([P, PACK * H], BF16, name="rounded", tag=tag, align_bytes=64)
             dst = tile[:].rearrange("p (t m i) -> p m i t", t=PACK, i=PACK)
-            src = raw[:].rearrange("p i (m t) -> p m i t", t=PACK)
-            nc.scalar.copy(dst, src)
+            count = P // len(raw)
+            for n, part in enumerate(raw):
+                nc.scalar.copy(dst[:, count * n : count * (n + 1)], part[:].rearrange("p i (m t) -> p m i t", t=PACK))
             return tile
 
-        def quantize(rounded, width, name):
-            codes = keep.tile([P, width], U32, name=name + "_codes", align_bytes=64)
+        def quantize(rounded, width, name, tag):
+            codes = keep.tile([P, width], U32, name=name + "_codes", tag=tag, align_bytes=64)
             scales = keep.tile([P, width], U8, name=name + "_scales", align_bytes=64)
             nc.vector.quantize_mx(out=codes[:].bitcast(FP8X4), scales=scales[:], in_=rounded)
             return codes, scales
@@ -158,9 +172,9 @@ def tile_list_hub_wear_board_kernel(
             w4_word[:].rearrange("p (t m) -> p m t", t=PACK),
             w4_word_raw[:].rearrange("p (m t) -> p m t", t=PACK),
         )
-        w4_scale = deal_scales(nc.vector, w4_scale_raw, "w4_scale")
-        w3_q = quantize(round_weight(w3_raw, "rounded0")[:], H, "w3")
-        w5_q = quantize(round_weight(w5_raw, "rounded1")[:], H, "w5")
+        w4_scale = deal_scales(w4_scale_raw, "w4_scale")
+        w3_q = quantize(round_weight(w3_raw, "w3_rounded")[:], H, "w3", "v2_word_tab")
+        w5_q = quantize(round_weight(w5_raw, "w5_rounded")[:], H, "w5", "w5_codes")
 
         def product_v2(weight, t, name):
             acc = bank(name)
@@ -173,51 +187,51 @@ def tile_list_hub_wear_board_kernel(
 
         def place_h2(t, h2):
             nc.vector.tensor_tensor(h2, e_acc[t][:], larger[t][:], ALU.mult)
-            nc.vector.tensor_tensor(page[t][:].indirect(idx4[:]), h2, gain2[t][:], ALU.mult)
+            nc.vector.tensor_tensor(page[t][:].indirect(idx4[:]), h2, gain2[t], ALU.mult)
 
         e_acc, larger = [], []
         for t in range(PACK):
             c_acc = product_v2(w3_q, t, "c_acc")
             d_acc = product_v2((w4_word, w4_scale), t, "d_acc")
             e_acc.append(product_v2(w5_q, t, "e_acc"))
-            c_sb = work.tile([P, S], F32, name="c_sb", bufs=2)
-            nc.scalar.copy(c_sb[:], c_acc[:])
-            larger.append(work.tile([P, S], F32, name="larger"))
-            nc.vector.tensor_tensor(larger[t][:], d_acc[:], c_sb[:], ALU.max)
-            if t == 0:
-                h2_first = keep.tile([P, S], F32, name="h2_first")
-                place_h2(0, h2_first[:])
+            if t % 2 == 0:
+                c_pair = keep.tile([P, 2, S], F32, name="c_pair", tag="w5_raw_right", align_bytes=64)
+            nc.scalar.copy(c_pair[:, t % 2, :], c_acc[:])
+            larger.append(work.tile([P, S], F32, name="larger", align_bytes=64))
+            nc.vector.tensor_tensor(larger[t][:], d_acc[:], c_pair[:, t % 2, :], ALU.max)
+            if t < 2:
+                h2_early = keep.tile([P, S], F32, name="h2_early%d" % t)
+                place_h2(t, h2_early[:])
 
-        v_scale = [gather_scales(v_scale_tab, a, idx, "v_scale%d" % a) for a in range(2)]
-        w6_scale = deal_scales(nc.gpsimd, w6_scale_raw, "w6_scale")
-        w6_word = keep.tile([P, 2 * H], U8, name="w6_word", align_bytes=64)
-        nc.gpsimd.tensor_copy(
-            w6_word[:].rearrange("p (t m b) -> p t m b", t=PACK, b=2),
-            w6_word_raw[:].bitcast(U8).rearrange("p (m t b) -> p t m b", t=PACK, b=2),
-        )
+        v_scale = [gather_scales(v_scale_tab, 0, idx, "w3_rounded"), v_scale_second]
+        for quad in range(4):
+            nc.gpsimd.dma_start(
+                v_scale_second[QUAD * quad : QUAD * quad + 4, :].bitcast(I32),
+                v_scale[0][QUAD * quad + 4 : QUAD * quad + 8, :].bitcast(I32),
+            )
         v_word = [gather_words(v_word_tab[a], idx, "v_word%d" % a) for a in range(2)]
-        w1_q = [quantize(round_weight(w1_raw[a], "rounded%d" % a)[:], H, "w1_%d" % a) for a in range(2)]
+        w1_q = [quantize(round_weight(w1_raw[a], ["w3_raw", "w5_raw_left"][a])[:], H, "w1_%d" % a, "w1_codes%d" % a) for a in range(2)]
 
-        neg_b = []
+        neg_b_first = keep.tile([P, 2, H], F32, name="neg_b_first", tag="w1_raw1_right", align_bytes=64)
+        neg_b_last = keep.tile([P, 2, H], F32, name="neg_b_last")
+        neg_b = [neg_b_first[:, 0, :], neg_b_first[:, 1, :], neg_b_last[:, 0, :], neg_b_last[:, 1, :]]
         for jc in range(S // P):
-            b_acc = bank("b_acc")
+            b_acc = psum.tile([P, H], F32, name="b_acc", bufs=2)
             cols = slice(P * jc, P * (jc + 1))
             for a in range(2):
                 nc.tensor.matmul_mx(
                     out=b_acc[:], lhsT=v_word[a][:, cols].bitcast(FP8X4), lhsT_scale=v_scale[a][:, cols],
-                    rhs=w2_word[a][:].bitcast(U8).bitcast(FP4X4), rhs_scale=w2_scale[:, a, :],
+                    rhs=w2_word[:, a, :].bitcast(FP4X4), rhs_scale=w2_scale[:, a, :],
                     start=(a == 0), stop=(a == 1),
                 )
-            tile = work.tile([P, H], F32, name="neg_b", tag="neg_b_then_z", align_bytes=64)
             nc.scalar.activation(
-                tile[:].rearrange("j (t m) -> j t m", t=PACK),
+                neg_b[jc].rearrange("j (t m) -> j t m", t=PACK),
                 b_acc[:].rearrange("j (m t) -> j t m", t=PACK), ACT.Copy, scale=-1.0,
             )
-            neg_b.append(tile)
 
-        h2_rest = keep.tile([P, PACK - 1, S], F32, name="h2_rest", tag="rounded1", align_bytes=64)
-        for t in range(1, PACK):
-            place_h2(t, h2_rest[:, t - 1, :])
+        h2_late = keep.tile([P, 2, S], F32, name="h2_late", tag="w5_raw_left", align_bytes=64)
+        for t in range(2, PACK):
+            place_h2(t, h2_late[:, t - 2, :])
 
         def add_transposed(dst, first, second):
             nc.tensor.matmul(dst, first, ident[:], is_transpose=True, start=True, stop=False)
@@ -248,15 +262,15 @@ def tile_list_hub_wear_board_kernel(
             for jc in range(S // P):
                 blk = slice(P * jc, P * (jc + 1))
                 add_transposed(h1_acc[:, blk], sine[:, blk], neg_b[jc][:, cols])
-            h1_t = work.tile([P, S], F32, name="h1")
+            h1_t = keep.tile([P, S], F32, name="h1", tag="h1_%d" % t, align_bytes=64)
             nc.scalar.copy(h1_t[:], h1_acc[:])
             h1.append(h1_t)
 
         chunks = NREAD // CHUNK
         x = [keep.tile([P, NREAD], F32, name="x%d" % t) for t in range(PACK)]
-        z = [work.tile([P, CHUNK, PACK], BF16, name="z", tag="neg_b_then_z", align_bytes=64) for c in range(chunks)]
+        z = [work.tile([P, CHUNK, PACK], BF16, name="z", tag="larger", align_bytes=64) for c in range(chunks)]
         for t in range(PACK):
-            nc.vector.tensor_tensor(page[t][:].indirect(idx3[:]), h1[t][:], gain1[t][:], ALU.mult)
+            nc.vector.tensor_tensor(page[t][:].indirect(idx3[:]), h1[t][:], gain1[t], ALU.mult)
             piece = CHUNK if t == PACK - 1 else NREAD
             for j0 in range(0, NREAD, piece):
                 nc.vector.tensor_copy(
@@ -266,6 +280,18 @@ def tile_list_hub_wear_board_kernel(
                 nc.scalar.activation(
                     z[c][:, :, t], x[t][:, CHUNK * c : CHUNK * (c + 1)], ACT.Copy, scale=gr_col[:, t : t + 1]
                 )
+
+        w6_dealt = keep.tile([P, 3 * H], U8, name="w6_dealt", tag="h1_0", align_bytes=64)
+        w6_word = w6_dealt[:, 0 : 2 * H]
+        w6_scale = w6_dealt[:, 2 * H : 3 * H]
+        nc.gpsimd.tensor_copy(
+            w6_word.rearrange("p (t m b) -> p t m b", t=PACK, b=2),
+            w6_word_raw[:].bitcast(U8).rearrange("p (m t b) -> p t m b", t=PACK, b=2),
+        )
+        nc.gpsimd.tensor_copy(
+            w6_scale.rearrange("p (t m) -> p t m", t=PACK),
+            w6_scale_raw[:, 0, :].rearrange("p (m t) -> p t m", t=PACK),
+        )
 
         z_codes = [keep.tile([P, 512], U32, name="z_codes%d" % h, align_bytes=64) for h in range(2)]
         z_scales = [keep.tile([P, 512], U8, name="z_scales%d" % h, align_bytes=64) for h in range(2)]

@@ -21,6 +21,8 @@ ACT = mybir.ActivationFunctionType
 P = 128
 PACK = 4
 QUAD = 32
+TILES = H // P
+HALF = H // 2
 CHUNK = 256
 ROUNDER = 1.5 * 2.0**23
 
@@ -32,223 +34,201 @@ def tile_list_hub_wear_board_kernel(
     nc = tc.nc
     with ExitStack() as ctx:
         keep = ctx.enter_context(tc.tile_pool(name="keep", bufs=1))
-        work = ctx.enter_context(tc.tile_pool(name="work", bufs=4))
+        work = ctx.enter_context(tc.tile_pool(name="work", bufs=2))
         psum = ctx.enter_context(tc.psum_pool(name="psum", bufs=5))
 
         def bank(name):
             return psum.tile([P, 512], F32, name=name, tag="bank")
 
-        def load_list(src, name):
-            tile = keep.tile(list(src.shape), U16, name=name)
+        def load(src, dtype, name):
+            tile = keep.tile(list(src.shape), dtype, name=name, align_bytes=64)
             nc.sync.dma_start(tile[:], src)
             return tile
 
-        def load_words(src, name, queue):
-            tile = keep.tile([P, src.shape[1] // 4], I32, name=name, align_bytes=64)
-            queue.dma_start(tile[:], src.bitcast(I32))
+        def load_words(src, name):
+            return load(src.bitcast(I32), I32, name)
+
+        def zeroed_bytes(engine, shape, name):
+            tile = keep.tile(shape, U8, name=name, align_bytes=64)
+            engine.memset(tile[:].bitcast(I32), 0)
             return tile
 
-        def scale_tile(src, name):
-            tile = keep.tile([P, src.shape[0], src.shape[2]], U8, name=name, align_bytes=64)
-            nc.vector.memset(tile[:].bitcast(I32), 0)
-            return tile
-
-        def load_scales(tile, src, queue):
+        def load_scales(tile, src):
             for quad in range(4):
-                queue.dma_start(
+                nc.sync.dma_start(
                     tile[QUAD * quad : QUAD * quad + 4].bitcast(I32),
                     src[:, 4 * quad : 4 * quad + 4, :].rearrange("a q c -> q a c").bitcast(I32),
                 )
 
-        def load_weight(rows, c0, c1, name):
-            tile = keep.tile([P, PACK, c1 - c0], F32, name=name, align_bytes=64)
-            nc.sync.dma_start(tile[:], rows.rearrange("(p i) c -> p i c", i=PACK)[:, :, c0:c1])
-            return tile
+        def load_weight(rows, half, name):
+            by_word = rows.rearrange("(p i) c -> p i c", i=PACK)
+            return load(by_word[:, :, HALF * half : HALF * (half + 1)], F32, "%s_raw%d" % (name, half))
 
-        def load_gain(src, t0, t1, name):
-            tile = keep.tile([P, t1 - t0, S], F32, name="%s_%d" % (name, t0))
-            rows = src.rearrange("(q t) j -> q t j", t=PACK)[:, t0:t1, :]
-            for quad in range(4):
-                nc.sync.dma_start(tile[QUAD * quad : QUAD * (quad + 1)], rows)
-            return [tile[:, n, :] for n in range(t1 - t0)]
+        def load_page(b):
+            return load(page0[P * b : P * (b + 1), :], F32, "page%d" % b)
 
-        def load_page(t):
-            tile = keep.tile([P, T2], F32, name="page%d" % t)
-            nc.sync.dma_start(tile[:], page0.rearrange("(p t) c -> t p c", t=PACK)[t])
-            return tile
+        v2_scale_tab = zeroed_bytes(nc.gpsimd, [P, 1, T3], "v2_scale_tab")
+        v_scale_tab = zeroed_bytes(nc.vector, [P, T], "v_scale_tab")
+        w4_scale = zeroed_bytes(nc.vector, [P, 1, H], "w4_scale")
+        w2_scale = zeroed_bytes(nc.vector, [P, 2, H], "w2_scale")
+        w6_scale = zeroed_bytes(nc.vector, [P, 1, H], "w6_scale")
+        v_scale_second = zeroed_bytes(nc.vector, [P, S], "v_scale_second")
 
         warm = keep.tile([P, 2], F32, name="warm")
-        nc.vector.memset(warm[:, 0:1], 0.0)
+        nc.gpsimd.memset(warm[:, 0:1], 0.0)
         nc.scalar.activation(warm[:, 1:2], warm[:, 0:1], ACT.Silu)
 
-        v_scale_tab = keep.tile([P, 1, T], U8, name="v_scale_tab", align_bytes=64)
-        nc.vector.memset(v_scale_tab[:].bitcast(I32), 0)
-        v2_scale_tab = scale_tile(tab2_scales, "v2_scale_tab")
-        w4_scale_raw = scale_tile(w4_scales, "w4_scale_raw")
-        w6_scale_raw = scale_tile(w6_scales, "w6_scale_raw")
-        w2_scale = scale_tile(w2_scales, "w2_scale")
-        v_scale_second = keep.tile([P, S], U8, name="v_scale_second", align_bytes=64)
-        nc.vector.memset(v_scale_second[:].bitcast(I32), 0)
-
+        idx2 = load(offs2, U16, "idx2")
+        v2_word_tab = load_words(tab2_words[0].rearrange("p c i -> p (c i)"), "v2_word_tab")
+        load_scales(v2_scale_tab, tab2_scales)
+        w3_raw = [load_weight(w3, 0, "w3")]
+        w5_raw = [load_weight(w5, 0, "w5")]
+        w4_word = load_words(w4_words[0].rearrange("p c i -> p (c i)"), "w4_word")
+        idx = load(offs, U16, "idx")
         for quad in range(4):
-            nc.gpsimd.dma_start(
-                v_scale_tab[QUAD * quad : QUAD * quad + 8, 0, :].bitcast(I32),
+            nc.sync.dma_start(
+                v_scale_tab[QUAD * quad : QUAD * quad + 8, :].bitcast(I32),
                 tab_scales[:, 4 * quad : 4 * quad + 4, :].bitcast(I32),
             )
-
-        idx2 = load_list(offs2, "idx2")
-        idx = load_list(offs, "idx")
-        w3_raw = [load_weight(w3, 0, H, "w3_raw")]
-        load_scales(v2_scale_tab, tab2_scales, nc.sync)
-        v2_word_tab = load_words(tab2_words[0].rearrange("p c i -> p (c i)"), "v2_word_tab", nc.sync)
-        w4_word_raw = load_words(w4_words[0].rearrange("p c i -> p (c i)"), "w4_word_raw", nc.sync)
-        w5_raw = [load_weight(w5, 0, H // 2, "w5_raw_left")]
-        load_scales(w4_scale_raw, w4_scales, nc.sync)
-        w5_raw.append(load_weight(w5, H // 2, H, "w5_raw_right"))
+        load_scales(w4_scale, w4_scales)
         page = [load_page(0)]
-        gain2 = load_gain(wg2, 0, 1, "gain2")
-        idx4 = load_list(offs4, "idx4")
-        v_word_tab = [
-            load_words(tab_words[a].rearrange("p c i -> p (c i)"), "v_word_tab%d" % a, nc.sync) for a in range(2)
+        gain2 = load(wg2, F32, "gain2")
+        idx4 = load(offs4, U16, "idx4")
+        page.append(load_page(1))
+        w3_raw.append(load_weight(w3, 1, "w3"))
+        w5_raw.append(load_weight(w5, 1, "w5"))
+        v_word_tab = [load_words(tab_words[a].rearrange("p c i -> p (c i)"), "v_word_tab%d" % a) for a in range(2)]
+        w2_word = load_words(w2_words.rearrange("a p c -> p a c"), "w2_word")
+        load_scales(w2_scale, w2_scales)
+        w1_raw = [
+            [load_weight(w1[512 * a : 512 * (a + 1), :], half, "w1_pass%d" % a) for a in range(2)] for half in range(2)
         ]
-        w1_raw = [[load_weight(w1[0:512, :], 0, H, "w1_raw0")]]
-        w2_word = keep.tile([P, 2, 2 * H], U8, name="w2_word", align_bytes=64)
-        nc.sync.dma_start(w2_word[:].bitcast(I32), w2_words.rearrange("a p c -> p a c").bitcast(I32))
-        load_scales(w2_scale, w2_scales, nc.sync)
-        w1_raw.append([
-            load_weight(w1[512:1024, :], 0, H // 2, "w1_raw1_left"),
-            load_weight(w1[512:1024, :], H // 2, H, "w1_raw1_right"),
-        ])
-        for t in range(1, PACK):
-            page.append(load_page(t))
-            gain2 = gain2 + load_gain(wg2, t, t + 1, "gain2")
-        idx3 = load_list(offs3, "idx3")
-        idx5 = load_list(offs5, "idx5")
-        gr_col = keep.tile([P, PACK], F32, name="gr_col")
-        nc.sync.dma_start(gr_col[:], gr.rearrange("(p t) -> p t", t=PACK))
-        gain1 = load_gain(wg1, 0, 2, "gain1") + load_gain(wg1, 2, 3, "gain1") + load_gain(wg1, 3, 4, "gain1")
-        w6_word_raw = load_words(w6_words[0], "w6_word_raw", nc.sync)
-        load_scales(w6_scale_raw, w6_scales, nc.sync)
+        idx3 = load(offs3, U16, "idx3")
+        idx5 = load(offs5, U16, "idx5")
+        page = page + [load_page(2), load_page(3)]
+        gain1 = load(wg1, F32, "gain1")
+        w6_word = load_words(w6_words[0], "w6_word")
+        load_scales(w6_scale, w6_scales)
+        with nc.allow_non_contiguous_dma(reason="one factor for each partition and row tile"):
+            gr_col = load(gr.rearrange("(b p) -> p b", p=P), F32, "gr_col")
 
         ident = keep.tile([P, P], F32, name="ident")
         make_identity(nc, ident[:])
+        ident_bf = keep.tile([P, P], BF16, name="ident_bf")
+        make_identity(nc, ident_bf[:])
 
-        def gather_words(table, lst, name):
-            tile = keep.tile([P, S], U32, name=name, align_bytes=64)
-            nc.vector.tensor_copy(tile[:], table[:].bitcast(U32).indirect(lst[:]))
+        def gather(window, lst, dtype, tag):
+            tile = keep.tile([P, S], dtype, name="picked", tag=tag, align_bytes=64)
+            nc.vector.tensor_copy(tile[:], window.indirect(lst[:]))
             return tile
 
-        def gather_scales(table, a, lst, tag):
-            tile = keep.tile([P, S], U8, name="picked_scales", tag=tag, align_bytes=64)
-            nc.vector.tensor_copy(tile[:], table[:, a, :].indirect(lst[:]))
-            return tile
-
-        def deal_scales(raw, name):
-            tile = keep.tile([P, H], U8, name=name, align_bytes=64)
-            nc.vector.tensor_copy(
-                tile[:].rearrange("p (t m) -> p t m", t=PACK),
-                raw[:, 0, :].rearrange("p (m t) -> p t m", t=PACK),
+        def quantize_weight(raw, name, rounded_tag, codes_tag):
+            rounded = keep.tile([P, HALF, PACK], BF16, name="rounded", tag=rounded_tag, align_bytes=64)
+            nc.scalar.copy(
+                rounded[:].rearrange("p (c n) i -> p c i n", n=4), raw[:].rearrange("p i (c n) -> p c i n", n=4)
             )
-            return tile
-
-        def round_weight(raw, tag):
-            tile = keep.tile([P, PACK * H], BF16, name="rounded", tag=tag, align_bytes=64)
-            dst = tile[:].rearrange("p (t m i) -> p m i t", t=PACK, i=PACK)
-            count = P // len(raw)
-            for n, part in enumerate(raw):
-                nc.scalar.copy(dst[:, count * n : count * (n + 1)], part[:].rearrange("p i (m t) -> p m i t", t=PACK))
-            return tile
-
-        def quantize(rounded, width, name, tag):
-            codes = keep.tile([P, width], U32, name=name + "_codes", tag=tag, align_bytes=64)
-            scales = keep.tile([P, width], U8, name=name + "_scales", align_bytes=64)
-            nc.vector.quantize_mx(out=codes[:].bitcast(FP8X4), scales=scales[:], in_=rounded)
+            codes = keep.tile([P, HALF], U32, name="codes", tag=codes_tag, align_bytes=64)
+            scales = keep.tile([P, HALF], U8, name=name + "_scales", align_bytes=64)
+            nc.vector.quantize_mx(out=codes[:].bitcast(FP8X4), scales=scales[:], in_=rounded[:].rearrange("p c i -> p (c i)"))
             return codes, scales
 
-        v2_scale = gather_scales(v2_scale_tab, 0, idx2, "v2_scale")
-        v2_word = gather_words(v2_word_tab, idx2, "v2_word")
-        w4_word = keep.tile([P, H], I32, name="w4_word", align_bytes=64)
-        nc.vector.tensor_copy(
-            w4_word[:].rearrange("p (t m) -> p m t", t=PACK),
-            w4_word_raw[:].rearrange("p (m t) -> p m t", t=PACK),
-        )
-        w4_scale = deal_scales(w4_scale_raw, "w4_scale")
-        w3_q = quantize(round_weight(w3_raw, "w3_rounded")[:], H, "w3", "v2_word_tab")
-        w5_q = quantize(round_weight(w5_raw, "w5_rounded")[:], H, "w5", "w5_codes")
+        def stationary(quantized, b):
+            cols = slice(P * (b % 2), P * (b % 2 + 1))
+            return quantized[0][:, cols].bitcast(FP8X4), quantized[1][:, cols]
 
-        def product_v2(weight, t, name):
+        v2_word = gather(v2_word_tab[:].bitcast(U32), idx2, U32, "v2_word")
+        v2_scale = gather(v2_scale_tab[:, 0, :], idx2, U8, "v2_scale")
+
+        def product_v2(codes, scales, name):
             acc = bank(name)
-            cols = slice(P * t, P * (t + 1))
             nc.tensor.matmul_mx(
-                out=acc[:], lhsT=weight[0][:, cols].bitcast(FP8X4), lhsT_scale=weight[1][:, cols],
+                out=acc[:], lhsT=codes, lhsT_scale=scales,
                 rhs=v2_word[:].bitcast(FP8X4), rhs_scale=v2_scale[:], start=True, stop=True,
             )
             return acc
 
-        def place_h2(t, h2):
-            nc.vector.tensor_tensor(h2, e_acc[t][:], larger[t][:], ALU.mult)
-            nc.vector.tensor_tensor(page[t][:].indirect(idx4[:]), h2, gain2[t], ALU.mult)
+        def products_v2(half, w3_q, w5_q):
+            pairs = []
+            for b in range(2 * half, 2 * half + 2):
+                cols = slice(P * b, P * (b + 1))
+                c_acc = product_v2(*stationary(w3_q, b), "c_acc")
+                d_acc = product_v2(w4_word[:, cols].bitcast(FP8X4), w4_scale[:, 0, cols], "d_acc")
+                e_acc = product_v2(*stationary(w5_q, b), "e_acc")
+                c_sb = keep.tile([P, S], F32, name="c_%d" % b, align_bytes=64)
+                nc.scalar.copy(c_sb[:], c_acc[:])
+                larger = work.tile([P, S], F32, name="larger")
+                nc.vector.tensor_tensor(larger[:], d_acc[:], c_sb[:], ALU.max)
+                pairs.append((larger, e_acc))
+            return pairs
 
-        e_acc, larger = [], []
-        for t in range(PACK):
-            c_acc = product_v2(w3_q, t, "c_acc")
-            d_acc = product_v2((w4_word, w4_scale), t, "d_acc")
-            e_acc.append(product_v2(w5_q, t, "e_acc"))
-            if t % 2 == 0:
-                c_pair = keep.tile([P, 2, S], F32, name="c_pair", tag="w5_raw_right", align_bytes=64)
-            nc.scalar.copy(c_pair[:, t % 2, :], c_acc[:])
-            larger.append(work.tile([P, S], F32, name="larger", align_bytes=64))
-            nc.vector.tensor_tensor(larger[t][:], d_acc[:], c_pair[:, t % 2, :], ALU.max)
-            if t < 2:
-                h2_early = keep.tile([P, S], F32, name="h2_early%d" % t)
-                place_h2(t, h2_early[:])
+        def place_h2(half, pairs, h2):
+            for n, (larger, e_acc) in enumerate(pairs):
+                nc.vector.tensor_tensor(h2[n], e_acc[:], larger[:], ALU.mult)
+            for n in range(2):
+                nc.vector.tensor_tensor(page[2 * half + n][:].indirect(idx4[:]), h2[n], gain2[:], ALU.mult)
 
-        v_scale = [gather_scales(v_scale_tab, 0, idx, "w3_rounded"), v_scale_second]
+        early = [
+            quantize_weight(w3_raw[0], "w3_0", "w3_0_rounded", "w3_0_codes"),
+            quantize_weight(w5_raw[0], "w5_0", "w5_0_rounded", "w5_0_codes"),
+        ]
+        v_scale = [gather(v_scale_tab[:], idx, U8, "w5_0_rounded"), v_scale_second]
+        h2_early = [keep.tile([P, S], F32, name="h2_%d" % b, align_bytes=64) for b in range(2)]
+        place_h2(0, products_v2(0, *early), [tile[:] for tile in h2_early])
         for quad in range(4):
-            nc.gpsimd.dma_start(
+            nc.scalar.dma_start(
                 v_scale_second[QUAD * quad : QUAD * quad + 4, :].bitcast(I32),
                 v_scale[0][QUAD * quad + 4 : QUAD * quad + 8, :].bitcast(I32),
             )
-        v_word = [gather_words(v_word_tab[a], idx, "v_word%d" % a) for a in range(2)]
-        w1_q = [quantize(round_weight(w1_raw[a], ["w3_raw", "w5_raw_left"][a])[:], H, "w1_%d" % a, "w1_codes%d" % a) for a in range(2)]
+        late_pairs = products_v2(
+            1,
+            quantize_weight(w3_raw[1], "w3_1", "c_0", "h2_0"),
+            quantize_weight(w5_raw[1], "w5_1", "c_1", "h2_1"),
+        )
 
-        neg_b_first = keep.tile([P, 2, H], F32, name="neg_b_first", tag="w1_raw1_right", align_bytes=64)
+        v_word = [gather(v_word_tab[a][:].bitcast(U32), idx, U32, "c_%d" % a) for a in range(2)]
+        w1_rounded_tags = [["v_word_tab0", "v_word_tab1"], ["w1_pass0_raw0", "v_word_tab0"]]
+        w1_q = [
+            [
+                quantize_weight(w1_raw[half][a], "w1_%d_%d" % (half, a), w1_rounded_tags[half][a], "w1_%d_%d_codes" % (half, a))
+                for a in range(2)
+            ]
+            for half in range(2)
+        ]
+        h2_late = keep.tile([P, 2, S], F32, name="h2_late", tag="v_word_tab1", align_bytes=64)
+        place_h2(1, late_pairs, [h2_late[:, 0, :], h2_late[:, 1, :]])
+
+        neg_b_first = keep.tile([P, 2, H], F32, name="neg_b_first", tag="w1_pass1_raw0", align_bytes=64)
         neg_b_last = keep.tile([P, 2, H], F32, name="neg_b_last")
         neg_b = [neg_b_first[:, 0, :], neg_b_first[:, 1, :], neg_b_last[:, 0, :], neg_b_last[:, 1, :]]
-        for jc in range(S // P):
-            b_acc = psum.tile([P, H], F32, name="b_acc", bufs=2)
-            cols = slice(P * jc, P * (jc + 1))
-            for a in range(2):
-                nc.tensor.matmul_mx(
-                    out=b_acc[:], lhsT=v_word[a][:, cols].bitcast(FP8X4), lhsT_scale=v_scale[a][:, cols],
-                    rhs=w2_word[:, a, :].bitcast(FP4X4), rhs_scale=w2_scale[:, a, :],
-                    start=(a == 0), stop=(a == 1),
-                )
-            nc.scalar.activation(
-                neg_b[jc].rearrange("j (t m) -> j t m", t=PACK),
-                b_acc[:].rearrange("j (m t) -> j t m", t=PACK), ACT.Copy, scale=-1.0,
-            )
 
-        h2_late = keep.tile([P, 2, S], F32, name="h2_late", tag="w5_raw_left", align_bytes=64)
-        for t in range(2, PACK):
-            place_h2(t, h2_late[:, t - 2, :])
+        def products_w2():
+            for jc in range(S // P):
+                b_acc = psum.tile([P, H], F32, name="b_acc", bufs=2)
+                cols = slice(P * jc, P * (jc + 1))
+                for a in range(2):
+                    nc.tensor.matmul_mx(
+                        out=b_acc[:], lhsT=v_word[a][:, cols].bitcast(FP8X4), lhsT_scale=v_scale[a][:, cols],
+                        rhs=w2_word[:, a, :].bitcast(FP4X4), rhs_scale=w2_scale[:, a, :],
+                        start=(a == 0), stop=(a == 1),
+                    )
+                nc.scalar.activation(neg_b[jc], b_acc[:], ACT.Copy, scale=-1.0)
 
         def add_transposed(dst, first, second):
             nc.tensor.matmul(dst, first, ident[:], is_transpose=True, start=True, stop=False)
             nc.tensor.matmul(dst, second, ident[:], is_transpose=True, start=False, stop=True)
 
         h1 = []
-        for t in range(PACK):
+        for b in range(TILES):
             a_acc = psum.tile([P, S], F32, name="a_acc", bufs=1)
-            cols = slice(P * t, P * (t + 1))
             for a in range(2):
+                codes, scales = stationary(w1_q[b // 2][a], b)
                 nc.tensor.matmul_mx(
-                    out=a_acc[:], lhsT=w1_q[a][0][:, cols].bitcast(FP8X4), lhsT_scale=w1_q[a][1][:, cols],
+                    out=a_acc[:], lhsT=codes, lhsT_scale=scales,
                     rhs=v_word[a][:].bitcast(FP8X4), rhs_scale=v_scale[a][:], start=(a == 0), stop=(a == 1),
                 )
-            turns = work.tile([P, S], F32, name="turns", bufs=2)
+            turns = work.tile([P, S], F32, name="turns")
             nc.scalar.activation(turns[:], a_acc[:], ACT.Copy, scale=1.0 / (2.0 * math.pi))
-            whole = work.tile([P, S], U32, name="whole", bufs=2)
+            whole = work.tile([P, S], U32, name="whole")
             nc.scalar.activation(whole[:], turns[:], ACT.Copy, bias=ROUNDER)
             neg_whole = work.tile([P, S], F32, name="neg_whole", bufs=1)
             nc.scalar.activation(neg_whole[:], whole[:], ACT.Copy, scale=-1.0, bias=ROUNDER)
@@ -256,64 +236,81 @@ def tile_list_hub_wear_board_kernel(
             for jc in range(S // P):
                 blk = slice(P * jc, P * (jc + 1))
                 add_transposed(frac_acc[:, blk], turns[:, blk], neg_whole[:, blk])
-            sine = work.tile([P, S], F32, name="sine", bufs=2)
+            if b == 0:
+                products_w2()
+            sine = work.tile([P, S], F32, name="sine")
             nc.scalar.activation(sine[:], frac_acc[:], ACT.Sin, scale=2.0 * math.pi)
             h1_acc = bank("h1_acc")
             for jc in range(S // P):
                 blk = slice(P * jc, P * (jc + 1))
-                add_transposed(h1_acc[:, blk], sine[:, blk], neg_b[jc][:, cols])
-            h1_t = keep.tile([P, S], F32, name="h1", tag="h1_%d" % t, align_bytes=64)
-            nc.scalar.copy(h1_t[:], h1_acc[:])
-            h1.append(h1_t)
+                add_transposed(h1_acc[:, blk], sine[:, blk], neg_b[jc][:, P * b : P * (b + 1)])
+            h1_b = keep.tile([P, S], F32, name="h1_%d" % b)
+            nc.scalar.copy(h1_b[:], h1_acc[:])
+            h1.append(h1_b)
 
-        chunks = NREAD // CHUNK
-        x = [keep.tile([P, NREAD], F32, name="x%d" % t) for t in range(PACK)]
-        z = [work.tile([P, CHUNK, PACK], BF16, name="z", tag="larger", align_bytes=64) for c in range(chunks)]
-        for t in range(PACK):
-            nc.vector.tensor_tensor(page[t][:].indirect(idx3[:]), h1[t][:], gain1[t], ALU.mult)
-            piece = CHUNK if t == PACK - 1 else NREAD
-            for j0 in range(0, NREAD, piece):
-                nc.vector.tensor_copy(
-                    x[t][:, j0 : j0 + piece], page[t][:].indirect(idx5[:, j0 // 16 : (j0 + piece) // 16])
-                )
-            for c in range(chunks):
-                nc.scalar.activation(
-                    z[c][:, :, t], x[t][:, CHUNK * c : CHUNK * (c + 1)], ACT.Copy, scale=gr_col[:, t : t + 1]
-                )
-
-        w6_dealt = keep.tile([P, 3 * H], U8, name="w6_dealt", tag="h1_0", align_bytes=64)
-        w6_word = w6_dealt[:, 0 : 2 * H]
-        w6_scale = w6_dealt[:, 2 * H : 3 * H]
-        nc.gpsimd.tensor_copy(
-            w6_word.rearrange("p (t m b) -> p t m b", t=PACK, b=2),
-            w6_word_raw[:].bitcast(U8).rearrange("p (m t b) -> p t m b", t=PACK, b=2),
-        )
-        nc.gpsimd.tensor_copy(
-            w6_scale.rearrange("p (t m) -> p t m", t=PACK),
-            w6_scale_raw[:, 0, :].rearrange("p (m t) -> p t m", t=PACK),
-        )
-
+        x = [keep.tile([P, NREAD], F32, name="x%d" % b) for b in range(TILES)]
+        turned = [keep.tile([P, 4, 2, P], F32, name="turned%d" % h) for h in range(2)]
         z_codes = [keep.tile([P, 512], U32, name="z_codes%d" % h, align_bytes=64) for h in range(2)]
         z_scales = [keep.tile([P, 512], U8, name="z_scales%d" % h, align_bytes=64) for h in range(2)]
-        for c in range(chunks):
-            cols = slice(CHUNK * (c % 2), CHUNK * (c % 2 + 1))
-            nc.vector.quantize_mx(
-                out=z_codes[c // 2][:, cols].bitcast(FP8X4), scales=z_scales[c // 2][:, cols],
-                in_=z[c][:].rearrange("p j t -> p (j t)"),
+
+        z_all = keep.tile([P, NREAD], BF16, name="z_all", tag="neg_b_last")
+
+        def read_page(b, j0, count):
+            nc.vector.tensor_copy(x[b][:, j0 : j0 + count], page[b][:].indirect(idx5[:, j0 // 16 : (j0 + count) // 16]))
+
+        def turn_z(b, j0, count):
+            z = z_all[:, j0 : j0 + count]
+            nc.scalar.activation(z, x[b][:, j0 : j0 + count], ACT.Copy, scale=gr_col[:, b : b + 1])
+            blocks = count // P
+            acc = psum.tile([P, blocks, P], BF16, name="z_turned", tag="bank")
+            for n in range(blocks):
+                nc.tensor.transpose(acc[:, n, :], z[:, P * n : P * (n + 1)], ident_bf[:])
+            first = (j0 % 512) // P
+            nc.scalar.copy(
+                turned[j0 // 512][:, first : first + blocks, :, QUAD * b : QUAD * (b + 1)],
+                acc[:].bitcast(F32).rearrange("j n (q u) -> j n u q", u=2),
             )
 
-        out_rows = out.rearrange("(p t) j -> t p j", t=PACK)
+        for b in range(TILES - 1):
+            nc.vector.tensor_tensor(page[b][:].indirect(idx3[:]), h1[b][:], gain1[:], ALU.mult)
+            read_page(b, 0, NREAD)
+            for h in range(2):
+                turn_z(b, 512 * h, 512)
+
+        last = TILES - 1
+        nc.vector.tensor_tensor(page[last][:].indirect(idx3[:]), h1[last][:], gain1[:], ALU.mult)
+        for j0 in range(0, NREAD, CHUNK):
+            read_page(last, j0, CHUNK)
+        for j0 in range(0, NREAD, CHUNK):
+            turn_z(last, j0, CHUNK)
+        for j0 in range(0, NREAD, CHUNK):
+            h, first = j0 // 512, (j0 % 512) // P
+            acc = psum.tile([P, 2, 2, P], F32, name="z_back", tag="bank")
+            for n in range(2):
+                for u in range(2):
+                    nc.tensor.transpose(acc[:, n, u, :], turned[h][:, first + n, u, :], ident[:])
+            grouped = keep.tile([P, 2, P, 2], F32, name="grouped%d" % j0, align_bytes=64)
+            if h == 0:
+                nc.vector.tensor_copy(grouped[:], acc[:].rearrange("p n u j -> p n j u"))
+            else:
+                nc.scalar.copy(grouped[:], acc[:].rearrange("p n u j -> p n j u"))
+            cols = slice(j0 % 512, j0 % 512 + CHUNK)
+            nc.vector.quantize_mx(
+                out=z_codes[h][:, cols].bitcast(FP8X4), scales=z_scales[h][:, cols],
+                in_=grouped[:].rearrange("p n j u -> p (n j u)").bitcast(BF16),
+            )
+
         for h in range(2):
             cols = slice(512 * h, 512 * (h + 1))
-            for t in range(PACK):
+            for b in range(TILES):
                 y_acc = bank("y_acc")
                 nc.tensor.matmul_mx(
                     out=y_acc[:],
-                    lhsT=w6_word[:, 2 * P * t : 2 * P * (t + 1)].bitcast(FP4X4),
-                    lhsT_scale=w6_scale[:, P * t : P * (t + 1)],
+                    lhsT=w6_word[:, 64 * b : 64 * (b + 1)].bitcast(FP4X4),
+                    lhsT_scale=w6_scale[:, 0, P * b : P * (b + 1)],
                     rhs=z_codes[h][:].bitcast(FP8X4), rhs_scale=z_scales[h][:], start=True, stop=True,
                 )
-                result = keep.tile([P, 512], F32, name="result%d_%d" % (h, t))
+                result = keep.tile([P, 512], F32, name="result%d_%d" % (h, b))
                 nc.scalar.activation(result[:], y_acc[:], ACT.Tanh)
-                nc.vector.tensor_tensor(result[:], result[:], x[t][:, cols], ALU.mult)
-                nc.sync.dma_start(out_rows[t][:, cols], result[:])
+                nc.vector.tensor_tensor(result[:], result[:], x[b][:, cols], ALU.mult)
+                nc.sync.dma_start(out[P * b : P * (b + 1), cols], result[:])

import math
from contextlib import ExitStack

import concourse.mybir as mybir
from concourse.masks import make_identity

K, L, H, T, T3, S, T2, NREAD = 1024, 512, 512, 2048, 1024, 512, 2048, 1024
FLOPS = 2 * (2 * K * H * S + 3 * L * H * S + H * H * NREAD)

F32 = mybir.dt.float32
BF16 = mybir.dt.bfloat16
I32 = mybir.dt.int32
U32 = mybir.dt.uint32
U16 = mybir.dt.uint16
U8 = mybir.dt.uint8
FP8X4 = mybir.dt.float8_e4m3fn_x4
FP4X4 = mybir.dt.float4_e2m1fn_x4
ALU = mybir.AluOpType
ACT = mybir.ActivationFunctionType

P = 128
PACK = 4
QUAD = 32
TILES = H // P
HALF = H // 2
CHUNK = 256
ROUNDER = 1.5 * 2.0**23


def tile_list_hub_wear_board_kernel(
    tc, tab_words, tab_scales, tab2_words, tab2_scales, offs, offs2, offs3, offs4, offs5,
    w1, w2_words, w2_scales, w3, w4_words, w4_scales, w5, w6_words, w6_scales, wg1, wg2, page0, gr, out,
):
    nc = tc.nc
    with ExitStack() as ctx:
        keep = ctx.enter_context(tc.tile_pool(name="keep", bufs=1))
        work = ctx.enter_context(tc.tile_pool(name="work", bufs=2))
        psum = ctx.enter_context(tc.psum_pool(name="psum", bufs=5))

        def bank(name):
            return psum.tile([P, 512], F32, name=name, tag="bank")

        def load(src, dtype, name):
            tile = keep.tile(list(src.shape), dtype, name=name, align_bytes=64)
            nc.sync.dma_start(tile[:], src)
            return tile

        def load_words(src, name):
            return load(src.bitcast(I32), I32, name)

        def zeroed_bytes(engine, shape, name):
            tile = keep.tile(shape, U8, name=name, align_bytes=64)
            engine.memset(tile[:].bitcast(I32), 0)
            return tile

        def load_scales(tile, src):
            for quad in range(4):
                nc.sync.dma_start(
                    tile[QUAD * quad : QUAD * quad + 4].bitcast(I32),
                    src[:, 4 * quad : 4 * quad + 4, :].rearrange("a q c -> q a c").bitcast(I32),
                )

        def load_weight(rows, half, name):
            by_word = rows.rearrange("(p i) c -> p i c", i=PACK)
            return load(by_word[:, :, HALF * half : HALF * (half + 1)], F32, "%s_raw%d" % (name, half))

        def load_page(b):
            return load(page0[P * b : P * (b + 1), :], F32, "page%d" % b)

        v2_scale_tab = zeroed_bytes(nc.gpsimd, [P, 1, T3], "v2_scale_tab")
        v_scale_tab = zeroed_bytes(nc.vector, [P, T], "v_scale_tab")
        w4_scale = zeroed_bytes(nc.vector, [P, 1, H], "w4_scale")
        w2_scale = zeroed_bytes(nc.vector, [P, 2, H], "w2_scale")
        w6_scale = zeroed_bytes(nc.vector, [P, 1, H], "w6_scale")
        v_scale_second = zeroed_bytes(nc.vector, [P, S], "v_scale_second")

        warm = keep.tile([P, 2], F32, name="warm")
        nc.gpsimd.memset(warm[:, 0:1], 0.0)
        nc.scalar.activation(warm[:, 1:2], warm[:, 0:1], ACT.Silu)

        idx2 = load(offs2, U16, "idx2")
        v2_word_tab = load_words(tab2_words[0].rearrange("p c i -> p (c i)"), "v2_word_tab")
        load_scales(v2_scale_tab, tab2_scales)
        w3_raw = [load_weight(w3, 0, "w3")]
        w5_raw = [load_weight(w5, 0, "w5")]
        w4_word = load_words(w4_words[0].rearrange("p c i -> p (c i)"), "w4_word")
        idx = load(offs, U16, "idx")
        for quad in range(4):
            nc.sync.dma_start(
                v_scale_tab[QUAD * quad : QUAD * quad + 8, :].bitcast(I32),
                tab_scales[:, 4 * quad : 4 * quad + 4, :].bitcast(I32),
            )
        load_scales(w4_scale, w4_scales)
        page = [load_page(0)]
        gain2 = load(wg2, F32, "gain2")
        idx4 = load(offs4, U16, "idx4")
        page.append(load_page(1))
        w3_raw.append(load_weight(w3, 1, "w3"))
        w5_raw.append(load_weight(w5, 1, "w5"))
        v_word_tab = [load_words(tab_words[a].rearrange("p c i -> p (c i)"), "v_word_tab%d" % a) for a in range(2)]
        w2_word = load_words(w2_words.rearrange("a p c -> p a c"), "w2_word")
        load_scales(w2_scale, w2_scales)
        w1_raw = [
            [load_weight(w1[512 * a : 512 * (a + 1), :], half, "w1_pass%d" % a) for a in range(2)] for half in range(2)
        ]
        idx3 = load(offs3, U16, "idx3")
        idx5 = load(offs5, U16, "idx5")
        page = page + [load_page(2), load_page(3)]
        gain1 = load(wg1, F32, "gain1")
        w6_word = load_words(w6_words[0], "w6_word")
        load_scales(w6_scale, w6_scales)
        with nc.allow_non_contiguous_dma(reason="one factor for each partition and row tile"):
            gr_col = load(gr.rearrange("(b p) -> p b", p=P), F32, "gr_col")

        ident = keep.tile([P, P], F32, name="ident")
        make_identity(nc, ident[:])
        ident_bf = keep.tile([P, P], BF16, name="ident_bf")
        make_identity(nc, ident_bf[:])

        def gather(window, lst, dtype, tag):
            tile = keep.tile([P, S], dtype, name="picked", tag=tag, align_bytes=64)
            nc.vector.tensor_copy(tile[:], window.indirect(lst[:]))
            return tile

        def quantize_weight(raw, name, rounded_tag, codes_tag):
            rounded = keep.tile([P, HALF, PACK], BF16, name="rounded", tag=rounded_tag, align_bytes=64)
            nc.scalar.copy(
                rounded[:].rearrange("p (c n) i -> p c i n", n=4), raw[:].rearrange("p i (c n) -> p c i n", n=4)
            )
            codes = keep.tile([P, HALF], U32, name="codes", tag=codes_tag, align_bytes=64)
            scales = keep.tile([P, HALF], U8, name=name + "_scales", align_bytes=64)
            nc.vector.quantize_mx(out=codes[:].bitcast(FP8X4), scales=scales[:], in_=rounded[:].rearrange("p c i -> p (c i)"))
            return codes, scales

        def stationary(quantized, b):
            cols = slice(P * (b % 2), P * (b % 2 + 1))
            return quantized[0][:, cols].bitcast(FP8X4), quantized[1][:, cols]

        v2_word = gather(v2_word_tab[:].bitcast(U32), idx2, U32, "v2_word")
        v2_scale = gather(v2_scale_tab[:, 0, :], idx2, U8, "v2_scale")

        def product_v2(codes, scales, name):
            acc = bank(name)
            nc.tensor.matmul_mx(
                out=acc[:], lhsT=codes, lhsT_scale=scales,
                rhs=v2_word[:].bitcast(FP8X4), rhs_scale=v2_scale[:], start=True, stop=True,
            )
            return acc

        def products_v2(half, w3_q, w5_q):
            pairs = []
            for b in range(2 * half, 2 * half + 2):
                cols = slice(P * b, P * (b + 1))
                c_acc = product_v2(*stationary(w3_q, b), "c_acc")
                d_acc = product_v2(w4_word[:, cols].bitcast(FP8X4), w4_scale[:, 0, cols], "d_acc")
                e_acc = product_v2(*stationary(w5_q, b), "e_acc")
                c_sb = keep.tile([P, S], F32, name="c_%d" % b, align_bytes=64)
                nc.scalar.copy(c_sb[:], c_acc[:])
                larger = work.tile([P, S], F32, name="larger")
                nc.vector.tensor_tensor(larger[:], d_acc[:], c_sb[:], ALU.max)
                pairs.append((larger, e_acc))
            return pairs

        def place_h2(half, pairs, h2):
            for n, (larger, e_acc) in enumerate(pairs):
                nc.vector.tensor_tensor(h2[n], e_acc[:], larger[:], ALU.mult)
            for n in range(2):
                nc.vector.tensor_tensor(page[2 * half + n][:].indirect(idx4[:]), h2[n], gain2[:], ALU.mult)

        early = [
            quantize_weight(w3_raw[0], "w3_0", "w3_0_rounded", "w3_0_codes"),
            quantize_weight(w5_raw[0], "w5_0", "w5_0_rounded", "w5_0_codes"),
        ]
        v_scale = [gather(v_scale_tab[:], idx, U8, "w5_0_rounded"), v_scale_second]
        h2_early = [keep.tile([P, S], F32, name="h2_%d" % b, align_bytes=64) for b in range(2)]
        place_h2(0, products_v2(0, *early), [tile[:] for tile in h2_early])
        for quad in range(4):
            nc.scalar.dma_start(
                v_scale_second[QUAD * quad : QUAD * quad + 4, :].bitcast(I32),
                v_scale[0][QUAD * quad + 4 : QUAD * quad + 8, :].bitcast(I32),
            )
        late_pairs = products_v2(
            1,
            quantize_weight(w3_raw[1], "w3_1", "c_0", "h2_0"),
            quantize_weight(w5_raw[1], "w5_1", "c_1", "h2_1"),
        )

        v_word = [gather(v_word_tab[a][:].bitcast(U32), idx, U32, "c_%d" % a) for a in range(2)]
        w1_rounded_tags = [["v_word_tab0", "v_word_tab1"], ["w1_pass0_raw0", "v_word_tab0"]]
        w1_q = [
            [
                quantize_weight(w1_raw[half][a], "w1_%d_%d" % (half, a), w1_rounded_tags[half][a], "w1_%d_%d_codes" % (half, a))
                for a in range(2)
            ]
            for half in range(2)
        ]
        h2_late = keep.tile([P, 2, S], F32, name="h2_late", tag="v_word_tab1", align_bytes=64)
        place_h2(1, late_pairs, [h2_late[:, 0, :], h2_late[:, 1, :]])

        neg_b_first = keep.tile([P, 2, H], F32, name="neg_b_first", tag="w1_pass1_raw0", align_bytes=64)
        neg_b_last = keep.tile([P, 2, H], F32, name="neg_b_last")
        neg_b = [neg_b_first[:, 0, :], neg_b_first[:, 1, :], neg_b_last[:, 0, :], neg_b_last[:, 1, :]]

        def products_w2():
            for jc in range(S // P):
                b_acc = psum.tile([P, H], F32, name="b_acc", bufs=2)
                cols = slice(P * jc, P * (jc + 1))
                for a in range(2):
                    nc.tensor.matmul_mx(
                        out=b_acc[:], lhsT=v_word[a][:, cols].bitcast(FP8X4), lhsT_scale=v_scale[a][:, cols],
                        rhs=w2_word[:, a, :].bitcast(FP4X4), rhs_scale=w2_scale[:, a, :],
                        start=(a == 0), stop=(a == 1),
                    )
                nc.scalar.activation(neg_b[jc], b_acc[:], ACT.Copy, scale=-1.0)

        def add_transposed(dst, first, second):
            nc.tensor.matmul(dst, first, ident[:], is_transpose=True, start=True, stop=False)
            nc.tensor.matmul(dst, second, ident[:], is_transpose=True, start=False, stop=True)

        h1 = []
        for b in range(TILES):
            a_acc = psum.tile([P, S], F32, name="a_acc", bufs=1)
            for a in range(2):
                codes, scales = stationary(w1_q[b // 2][a], b)
                nc.tensor.matmul_mx(
                    out=a_acc[:], lhsT=codes, lhsT_scale=scales,
                    rhs=v_word[a][:].bitcast(FP8X4), rhs_scale=v_scale[a][:], start=(a == 0), stop=(a == 1),
                )
            turns = work.tile([P, S], F32, name="turns")
            nc.scalar.activation(turns[:], a_acc[:], ACT.Copy, scale=1.0 / (2.0 * math.pi))
            whole = work.tile([P, S], U32, name="whole")
            nc.scalar.activation(whole[:], turns[:], ACT.Copy, bias=ROUNDER)
            neg_whole = work.tile([P, S], F32, name="neg_whole", bufs=1)
            nc.scalar.activation(neg_whole[:], whole[:], ACT.Copy, scale=-1.0, bias=ROUNDER)
            frac_acc = bank("frac_acc")
            for jc in range(S // P):
                blk = slice(P * jc, P * (jc + 1))
                add_transposed(frac_acc[:, blk], turns[:, blk], neg_whole[:, blk])
            if b == 0:
                products_w2()
            sine = work.tile([P, S], F32, name="sine")
            nc.scalar.activation(sine[:], frac_acc[:], ACT.Sin, scale=2.0 * math.pi)
            h1_acc = bank("h1_acc")
            for jc in range(S // P):
                blk = slice(P * jc, P * (jc + 1))
                add_transposed(h1_acc[:, blk], sine[:, blk], neg_b[jc][:, P * b : P * (b + 1)])
            h1_b = keep.tile([P, S], F32, name="h1_%d" % b)
            nc.scalar.copy(h1_b[:], h1_acc[:])
            h1.append(h1_b)

        x = [keep.tile([P, NREAD], F32, name="x%d" % b) for b in range(TILES)]
        turned = [keep.tile([P, 4, 2, P], F32, name="turned%d" % h) for h in range(2)]
        z_codes = [keep.tile([P, 512], U32, name="z_codes%d" % h, align_bytes=64) for h in range(2)]
        z_scales = [keep.tile([P, 512], U8, name="z_scales%d" % h, align_bytes=64) for h in range(2)]

        z_all = keep.tile([P, NREAD], BF16, name="z_all", tag="neg_b_last")

        def read_page(b, j0, count):
            nc.vector.tensor_copy(x[b][:, j0 : j0 + count], page[b][:].indirect(idx5[:, j0 // 16 : (j0 + count) // 16]))

        def turn_z(b, j0, count):
            z = z_all[:, j0 : j0 + count]
            nc.scalar.activation(z, x[b][:, j0 : j0 + count], ACT.Copy, scale=gr_col[:, b : b + 1])
            blocks = count // P
            acc = psum.tile([P, blocks, P], BF16, name="z_turned", tag="bank")
            for n in range(blocks):
                nc.tensor.transpose(acc[:, n, :], z[:, P * n : P * (n + 1)], ident_bf[:])
            first = (j0 % 512) // P
            nc.scalar.copy(
                turned[j0 // 512][:, first : first + blocks, :, QUAD * b : QUAD * (b + 1)],
                acc[:].bitcast(F32).rearrange("j n (q u) -> j n u q", u=2),
            )

        for b in range(TILES - 1):
            nc.vector.tensor_tensor(page[b][:].indirect(idx3[:]), h1[b][:], gain1[:], ALU.mult)
            read_page(b, 0, NREAD)
            for h in range(2):
                turn_z(b, 512 * h, 512)

        last = TILES - 1
        nc.vector.tensor_tensor(page[last][:].indirect(idx3[:]), h1[last][:], gain1[:], ALU.mult)
        for j0 in range(0, NREAD, CHUNK):
            read_page(last, j0, CHUNK)
        for j0 in range(0, NREAD, CHUNK):
            turn_z(last, j0, CHUNK)
        for j0 in range(0, NREAD, CHUNK):
            h, first = j0 // 512, (j0 % 512) // P
            acc = psum.tile([P, 2, 2, P], F32, name="z_back", tag="bank")
            for n in range(2):
                for u in range(2):
                    nc.tensor.transpose(acc[:, n, u, :], turned[h][:, first + n, u, :], ident[:])
            grouped = keep.tile([P, 2, P, 2], F32, name="grouped%d" % j0, align_bytes=64)
            if h == 0:
                nc.vector.tensor_copy(grouped[:], acc[:].rearrange("p n u j -> p n j u"))
            else:
                nc.scalar.copy(grouped[:], acc[:].rearrange("p n u j -> p n j u"))
            cols = slice(j0 % 512, j0 % 512 + CHUNK)
            nc.vector.quantize_mx(
                out=z_codes[h][:, cols].bitcast(FP8X4), scales=z_scales[h][:, cols],
                in_=grouped[:].rearrange("p n j u -> p (n j u)").bitcast(BF16),
            )

        for h in range(2):
            cols = slice(512 * h, 512 * (h + 1))
            for b in range(TILES):
                y_acc = bank("y_acc")
                nc.tensor.matmul_mx(
                    out=y_acc[:],
                    lhsT=w6_word[:, 64 * b : 64 * (b + 1)].bitcast(FP4X4),
                    lhsT_scale=w6_scale[:, 0, P * b : P * (b + 1)],
                    rhs=z_codes[h][:].bitcast(FP8X4), rhs_scale=z_scales[h][:], start=True, stop=True,
                )
                result = keep.tile([P, 512], F32, name="result%d_%d" % (h, b))
                nc.scalar.activation(result[:], y_acc[:], ACT.Tanh)
                nc.vector.tensor_tensor(result[:], result[:], x[b][:, cols], ALU.mult)
                nc.sync.dma_start(out[P * b : P * (b + 1), cols], result[:])
